import numpy as np
import ml_dtypes


def mxq(x, axis, fmt="e4m3"):
    dtype, down = {"e4m3": (ml_dtypes.float8_e4m3fn, 7), "e5m2": (ml_dtypes.float8_e5m2, 14)}[fmt]
    v = np.moveaxis(np.asarray(x, np.float32).astype(ml_dtypes.bfloat16).astype(np.float64), axis, -1)
    blocks = v.reshape(v.shape[:-1] + (-1, 32))
    amax = np.abs(blocks).max(-1, keepdims=True)
    byte = np.maximum(np.where(amax > 0, np.frexp(amax)[1] - 1 + 127, 0) - down, 1)
    scale = np.exp2(byte - 127.0)
    codes = (blocks / scale).astype(np.float32).astype(dtype).astype(np.float64)
    return np.moveaxis((codes * scale).reshape(v.shape), -1, axis)


WIDE = False


def mx_kscale(k):
    if not WIDE:
        return np.ones(k)
    levels = np.array([10, -10, 5, -5, 0])
    if k % 512:
        return np.exp2(np.random.permutation(np.resize(levels, k // 32))).repeat(32)
    a = np.empty((k // 512, 16))
    for p in range(k // 512):
        a[p, :8] = np.random.permutation(np.resize(levels, 8))
        for g in range(8):
            far = levels[np.abs(levels - a[p, g]) >= 10]
            a[p, g + 8] = far[np.random.randint(len(far))]
    return np.exp2(a.ravel()).repeat(32)


def f64(x):
    return np.asarray(x).astype(np.float64)


def striped(idx):
    return np.tile(idx.reshape(-1, 16).T, (8, 1)).astype(np.uint16)


def unstriped(offs):
    return offs[:16].T.reshape(-1).astype(np.int64)


def pack_weight(w):
    k, n = w.shape
    w = f64(np.asarray(w, np.float32).astype(ml_dtypes.bfloat16)).reshape(k // 32, 32, n)
    amax = np.abs(w).max(1)
    byte = np.clip(np.where(amax > 0, np.frexp(amax)[1] - 1 + 127 - 7, 1), 1, 254)
    scaled = (w * np.exp2(127.0 - byte)[:, None, :]).reshape(k, n).astype(np.float32)
    words = np.ascontiguousarray(scaled.reshape(k // 512, 128, 4, n).transpose(0, 1, 3, 2)).astype(ml_dtypes.float8_e4m3fn).view(np.uint8)
    return words, np.ascontiguousarray(byte.astype(np.uint8).reshape(k // 512, 16, n))


def unpack_weight(words, scales):
    g, p, n, _ = words.shape
    vals = np.ascontiguousarray(words).view(ml_dtypes.float8_e4m3fn).astype(np.float64) * np.repeat(np.exp2(scales.astype(np.float64) - 127.0), 8, axis=1)[..., None]
    return vals.transpose(0, 1, 3, 2).reshape(g * 512, n)


E2M1 = np.array([0.0, 0.5, 1.0, 1.5, 2.0, 3.0, 4.0, 6.0, -0.0, -0.5, -1.0, -1.5, -2.0, -3.0, -4.0, -6.0])


def pack_fp4(w):
    k, n = w.shape
    w = f64(np.asarray(w, np.float32).astype(ml_dtypes.bfloat16)).reshape(k // 32, 32, n)
    amax = np.abs(w).max(1)
    mant, ex = np.frexp(amax / 6.0)
    byte = np.clip(np.where(amax > 0, np.where(mant > 0.5, ex, ex - 1) + 127, 1), 1, 254)
    scaled = (w * np.exp2(127.0 - byte)[:, None, :]).reshape(k, n).astype(np.float32)
    c = np.ascontiguousarray(scaled.reshape(k // 512, 128, 4, n).transpose(0, 1, 3, 2)).astype(ml_dtypes.float4_e2m1fn).view(np.uint8) & 0xF
    words = (c[..., 0::2] | (c[..., 1::2] << 4)).reshape(k // 512, 128, 2 * n)
    return np.ascontiguousarray(words), np.ascontiguousarray(byte.astype(np.uint8).reshape(k // 512, 16, n))


def unpack_fp4(words, scales):
    g, _, n = scales.shape
    words = np.ascontiguousarray(words).reshape(g, 128, n, 2)
    nib = np.empty((g, 128, n, 4), np.uint8)
    nib[..., 0::2] = words & 0xF
    nib[..., 1::2] = words >> 4
    vals = E2M1[nib] * np.repeat(np.exp2(scales.astype(np.float64) - 127.0), 8, axis=1)[..., None]
    return vals.transpose(0, 1, 3, 2).reshape(g * 512, n)


def silu(v):
    return v / (1.0 + np.exp(-np.maximum(v, -700.0)))


K, T, S, H, N = 1024, 1024, 512, 512, 128
P = 2 ** 7


def setup_inputs():
    n = np.random.standard_normal
    s = mx_kscale(K)[:, None]
    u = mx_kscale(H)
    packed_xT = pack_weight(n((K, T)) * s)
    packed_w2 = pack_fp4(n((H, N)) / np.sqrt(H) / u[:, None])
    return {
        "x_words": packed_xT[0],
        "x_scales": packed_xT[1],
        "gate": np.tile(np.random.uniform(0.2, 1.0, T), (P, 1)).astype(np.float32),
        "w1": (n((K, H)) / np.sqrt(K) / s * u).astype(np.float32),
        "w2_words": packed_w2[0],
        "w2_scales": packed_w2[1],
        "offs": striped(np.random.permutation(T)[:S]),
    }


def reference(x_words, x_scales, gate, w1, w2_words, w2_scales, offs):
    xq = unpack_weight(x_words, x_scales)[:, unstriped(offs)]
    h = silu(mxq(f64(w1), 0, "e4m3").T @ xq)
    y = unpack_fp4(w2_words, w2_scales).T @ mxq(h, 0, "e4m3")
    g = f64(gate)[:1][:, unstriped(offs)]
    out = np.zeros((N, T))
    out[:, unstriped(offs)] = y * g
    return out

@@ -1,0 +1,224 @@
+from contextlib import ExitStack
+
+import concourse.mybir as mybir
+from concourse.masks import make_identity
+
+K, T, S, H, N = 1024, 1024, 512, 512, 128
+FLOPS = 2 * K * H * S + 2 * H * N * S
+
+F32 = mybir.dt.float32
+BF16 = mybir.dt.bfloat16
+I32 = mybir.dt.int32
+U32 = mybir.dt.uint32
+U16 = mybir.dt.uint16
+U8 = mybir.dt.uint8
+FP8X4 = mybir.dt.float8_e4m3fn_x4
+FP4X4 = mybir.dt.float4_e2m1fn_x4
+SILU = mybir.ActivationFunctionType.Silu
+MULT = mybir.AluOpType.mult
+
+P = 128
+PACK = 4
+PASSES = K // (P * PACK)
+BLOCK = 128
+BLOCKS = S // BLOCK
+HALF = H // 2
+MH = P // 2
+GC = T // P
+
+
+def tile_picked_modgate_mlpsilu_p_kernel(
+    tc, x_words, x_scales, gate, w1, w2_words, w2_scales, offs, out
+):
+    nc = tc.nc
+    with ExitStack() as ctx:
+        keep = ctx.enter_context(tc.tile_pool(name="keep", bufs=1))
+        psum = ctx.enter_context(tc.psum_pool(name="psum", bufs=1))
+
+        def sb(name, shape, dtype, tag=None):
+            return keep.tile(shape, dtype, name=name, tag=tag or name, align_bytes=64)
+
+        offsets = sb("offsets", [P, S // 16], U16)
+        nc.sync.dma_start(offsets[:], offs)
+
+        def entries(first, count):
+            return offsets[:, first // 16 : (first + count) // 16]
+
+        xs_all = sb("xs_all", [P, T], U8)
+        nc.vector.memset(xs_all[:].bitcast(I32), 0)
+        warm_in = sb("warm_in", [P, 1], F32)
+        warm_out = sb("warm_out", [P, 1], F32)
+        nc.gpsimd.memset(warm_in[:], 0.0)
+        nc.scalar.activation(warm_out[:], warm_in[:], SILU)
+        identity = sb("identity", [P, P], F32)
+        make_identity(nc, identity[:])
+
+        w2_plane = sb("w2_plane", [P, N], U8)
+        nc.vector.memset(w2_plane[:].bitcast(I32), 0)
+        window = sb("window", [P, T], F32)
+        nc.vector.memset(window[:], 0.0)
+
+        w1_raw = {}
+        xw_all = {}
+
+        def load_w1(z, half):
+            raw = sb("w1_raw%d%d" % (z, half), [P, PACK, HALF], F32)
+            rows = w1[z * P * PACK : (z + 1) * P * PACK, half * HALF : (half + 1) * HALF]
+            nc.sync.dma_start(raw[:], rows.rearrange("(p j) c -> p j c", j=PACK))
+            w1_raw[z, half] = raw
+
+        def load_x(z):
+            words = sb("xw_all%d" % z, [P, T], I32)
+            nc.sync.dma_start(words[:], x_words[z].rearrange("p n t -> p (n t)").bitcast(I32))
+            xw_all[z] = words
+
+        gate_col = sb("gate_col", [P, GC], F32)
+        nc.sync.dma_start(gate_col[:], gate[0].rearrange("(p c) -> p c", c=GC))
+        load_x(0)
+        w2_codes = sb("w2_codes", [P, 2 * N], U8)
+        nc.sync.dma_start(w2_codes[:].bitcast(I32), w2_words[0].bitcast(I32))
+        load_w1(0, 0)
+        for q in range(4):
+            nc.sync.dma_start(
+                xs_all[32 * q : 32 * q + 4 * PASSES, :].bitcast(I32),
+                x_scales[:, 4 * q : 4 * q + 4, :].bitcast(I32),
+            )
+        load_w1(0, 1)
+        load_w1(1, 0)
+        load_w1(1, 1)
+        load_x(1)
+        for q in range(4):
+            nc.sync.dma_start(
+                w2_plane[32 * q : 32 * q + 4, :].bitcast(I32),
+                w2_scales[0, 4 * q : 4 * q + 4, :].bitcast(I32),
+            )
+
+        gate_all = sb("gate_all", [P, T], F32)
+        for u in range(GC // PACK):
+            spread = psum.tile([P, PACK, P], F32, name="spread%d" % u, tag="y_bank%d" % (u + 2))
+            for c in range(PACK):
+                col = u * PACK + c
+                nc.tensor.transpose(
+                    spread[:, c, :], gate_col[:, col : col + 1].to_broadcast([P, P]), identity[:]
+                )
+            nc.scalar.copy(
+                gate_all[:].rearrange("p (n c) -> p n c", c=GC)[:, :, u * PACK : (u + 1) * PACK],
+                spread[:].rearrange("p c n -> p n c"),
+            )
+
+        xw = {}
+
+        def gather_x(z, first, count):
+            nc.vector.tensor_copy(
+                xw[z][:, first : first + count],
+                xw_all[z][:].bitcast(U32).indirect(entries(first, count)),
+            )
+
+        xw[0] = sb("xw0", [P, S], U32)
+        gather_x(0, 0, S)
+        g = sb("g", [P, S], F32, tag="xw_all0")
+        nc.vector.tensor_copy(g[:], gate_all[:].indirect(offsets[:]))
+        xs = sb("xs", [P, S], U8)
+        nc.vector.tensor_copy(xs[:], xs_all[:].indirect(offsets[:]))
+
+        w1_codes = {}
+        w1_plane = [sb("w1_plane%d" % z, [P, H], U8) for z in range(PASSES)]
+
+        def cast_w1(copy, grouped, z, half, pair):
+            src = w1_raw[z, half][:].rearrange("p j (m t) -> p m j t", t=PACK)
+            dst = grouped[:, :, half * MH : (half + 1) * MH, :]
+            copy(dst.rearrange("p t m j -> p m j t"), src[:, :, :, 2 * pair : 2 * pair + 2])
+
+        def quantize_w1(grouped, z, pair):
+            cols = slice(pair * HALF, (pair + 1) * HALF)
+            nc.vector.quantize_mx(
+                out=w1_codes[z][:, cols].bitcast(FP8X4),
+                scales=w1_plane[z][:, cols],
+                in_=grouped[:].rearrange("p t m j -> p (t m j)"),
+            )
+
+        banks = [psum.tile([P, PACK, BLOCK], F32, name="h_bank%d" % b) for b in range(BLOCKS)]
+
+        def first_product(z, b):
+            tokens = slice(b * BLOCK, (b + 1) * BLOCK)
+            for t in range(PACK):
+                cols = slice(t * P, (t + 1) * P)
+                nc.tensor.matmul_mx(
+                    out=banks[b][:, t, :],
+                    lhsT=w1_codes[z][:, cols].bitcast(FP8X4),
+                    lhsT_scale=w1_plane[z][:, cols],
+                    rhs=xw[z][:, tokens].bitcast(FP8X4),
+                    rhs_scale=xs[4 * z : P, tokens],
+                    start=(z == 0 and t == 0),
+                    stop=(z == PASSES - 1 and t == PACK - 1),
+                )
+
+        shape = [P, 2, P, PACK]
+        w1_codes[0] = sb("w1_codes0", [P, H], U32, tag="xs_all")
+        low0 = sb("low0", shape, BF16)
+        high0 = sb("high0", shape, BF16)
+        for half in range(2):
+            cast_w1(nc.scalar.copy, low0, 0, half, 0)
+            cast_w1(nc.scalar.copy, high0, 0, half, 1)
+        quantize_w1(low0, 0, 0)
+        quantize_w1(high0, 0, 1)
+        for b in range(BLOCKS):
+            first_product(0, b)
+        w1_codes[1] = sb("w1_codes1", [P, H], U32, tag="high0")
+        low1 = sb("low1", shape, BF16)
+        high1 = sb("high1", shape, BF16, tag="low0")
+        for half in range(2):
+            cast_w1(nc.scalar.copy, low1, 1, half, 0)
+            cast_w1(nc.vector.tensor_copy, high1, 1, half, 1)
+        quantize_w1(low1, 1, 0)
+        quantize_w1(high1, 1, 1)
+        xw[1] = sb("xw1", [P, S], U32, tag="low1")
+        for b in range(BLOCKS):
+            gather_x(1, b * BLOCK, BLOCK)
+            first_product(1, b)
+
+        h_codes = {}
+        h_plane = {}
+        y_sb = {}
+
+        def silu_quant(b):
+            h = sb("h%d" % b, [P, BLOCK, PACK], BF16, tag="h_codes%d" % (b - 2) if b >= 2 else None)
+            nc.scalar.activation(h[:], banks[b][:].rearrange("p t n -> p n t"), SILU)
+            h_codes[b] = sb("h_codes%d" % b, [P, BLOCK], U32)
+            h_plane[b] = sb("h_plane%d" % b, [P, BLOCK], U8)
+            nc.vector.quantize_mx(
+                out=h_codes[b][:].bitcast(FP8X4),
+                scales=h_plane[b][:],
+                in_=h[:].rearrange("p n t -> p (n t)"),
+            )
+
+        def second_product(b):
+            y = psum.tile([P, BLOCK], F32, name="y_bank%d" % b)
+            nc.tensor.matmul_mx(
+                out=y[:],
+                lhsT=w2_codes[:].bitcast(FP4X4),
+                lhsT_scale=w2_plane[:],
+                rhs=h_codes[b][:].bitcast(FP8X4),
+                rhs_scale=h_plane[b][:],
+                start=True,
+                stop=True,
+            )
+            y_sb[b] = sb("y_sb%d" % b, [P, BLOCK], F32)
+            nc.scalar.copy(y_sb[b][:], y[:])
+
+        def scatter(b):
+            nc.vector.tensor_tensor(
+                window[:].indirect(entries(b * BLOCK, BLOCK)),
+                y_sb[b][:],
+                g[:, b * BLOCK : (b + 1) * BLOCK],
+                MULT,
+            )
+
+        silu_quant(0)
+        silu_quant(1)
+        for b in range(BLOCKS):
+            second_product(b)
+            scatter(b)
+            if b + 2 < BLOCKS:
+                silu_quant(b + 2)
+        nc.sync.dma_start(out, window[:])

@@ -1,7 +1,6 @@
 from contextlib import ExitStack
 
 import concourse.mybir as mybir
-from concourse.masks import make_identity
 
 K, T, S, H, N = 1024, 1024, 512, 512, 128
 FLOPS = 2 * K * H * S + 2 * H * N * S
@@ -24,7 +23,6 @@ BLOCK = 128
 BLOCKS = S // BLOCK
 HALF = H // 2
 MH = P // 2
-GC = T // P
 
 
 def tile_picked_modgate_mlpsilu_p_kernel(
@@ -50,9 +48,6 @@ def tile_picked_modgate_mlpsilu_p_kernel(
         warm_out = sb("warm_out", [P, 1], F32)
         nc.gpsimd.memset(warm_in[:], 0.0)
         nc.scalar.activation(warm_out[:], warm_in[:], SILU)
-        identity = sb("identity", [P, P], F32)
-        make_identity(nc, identity[:])
-
         w2_plane = sb("w2_plane", [P, N], U8)
         nc.vector.memset(w2_plane[:].bitcast(I32), 0)
         window = sb("window", [P, T], F32)
@@ -72,11 +67,7 @@ def tile_picked_modgate_mlpsilu_p_kernel(
             nc.sync.dma_start(words[:], x_words[z].rearrange("p n t -> p (n t)").bitcast(I32))
             xw_all[z] = words
 
-        gate_col = sb("gate_col", [P, GC], F32)
-        nc.sync.dma_start(gate_col[:], gate[0].rearrange("(p c) -> p c", c=GC))
         load_x(0)
-        w2_codes = sb("w2_codes", [P, 2 * N], U8)
-        nc.sync.dma_start(w2_codes[:].bitcast(I32), w2_words[0].bitcast(I32))
         load_w1(0, 0)
         for q in range(4):
             nc.sync.dma_start(
@@ -87,23 +78,14 @@ def tile_picked_modgate_mlpsilu_p_kernel(
         load_w1(1, 0)
         load_w1(1, 1)
         load_x(1)
+        gate_all = sb("gate_all", [P, T], F32)
+        nc.sync.dma_start(gate_all[:], gate)
+        w2_codes = sb("w2_codes", [P, 2 * N], U8)
+        nc.sync.dma_start(w2_codes[:].bitcast(I32), w2_words[0].bitcast(I32))
         for q in range(4):
             nc.sync.dma_start(
                 w2_plane[32 * q : 32 * q + 4, :].bitcast(I32),
                 w2_scales[0, 4 * q : 4 * q + 4, :].bitcast(I32),
-            )
-
-        gate_all = sb("gate_all", [P, T], F32)
-        for u in range(GC // PACK):
-            spread = psum.tile([P, PACK, P], F32, name="spread%d" % u, tag="y_bank%d" % (u + 2))
-            for c in range(PACK):
-                col = u * PACK + c
-                nc.tensor.transpose(
-                    spread[:, c, :], gate_col[:, col : col + 1].to_broadcast([P, P]), identity[:]
-                )
-            nc.scalar.copy(
-                gate_all[:].rearrange("p (n c) -> p n c", c=GC)[:, :, u * PACK : (u + 1) * PACK],
-                spread[:].rearrange("p c n -> p n c"),
             )
 
         xw = {}
@@ -116,8 +98,6 @@ def tile_picked_modgate_mlpsilu_p_kernel(
 
         xw[0] = sb("xw0", [P, S], U32)
         gather_x(0, 0, S)
-        g = sb("g", [P, S], F32, tag="xw_all0")
-        nc.vector.tensor_copy(g[:], gate_all[:].indirect(offsets[:]))
         xs = sb("xs", [P, S], U8)
         nc.vector.tensor_copy(xs[:], xs_all[:].indirect(offsets[:]))
 
@@ -141,7 +121,7 @@ def tile_picked_modgate_mlpsilu_p_kernel(
 
         def first_product(z, b):
             tokens = slice(b * BLOCK, (b + 1) * BLOCK)
-            for t in range(PACK):
+            for t in (2, 3, 0, 1):
                 cols = slice(t * P, (t + 1) * P)
                 nc.tensor.matmul_mx(
                     out=banks[b][:, t, :],
@@ -149,30 +129,23 @@ def tile_picked_modgate_mlpsilu_p_kernel(
                     lhsT_scale=w1_plane[z][:, cols],
                     rhs=xw[z][:, tokens].bitcast(FP8X4),
                     rhs_scale=xs[4 * z : P, tokens],
-                    start=(z == 0 and t == 0),
-                    stop=(z == PASSES - 1 and t == PACK - 1),
+                    start=(z == 0 and t == 2),
+                    stop=(z == PASSES - 1 and t == 1),
                 )
 
-        shape = [P, 2, P, PACK]
-        w1_codes[0] = sb("w1_codes0", [P, H], U32, tag="xs_all")
-        low0 = sb("low0", shape, BF16)
-        high0 = sb("high0", shape, BF16)
-        for half in range(2):
-            cast_w1(nc.scalar.copy, low0, 0, half, 0)
-            cast_w1(nc.scalar.copy, high0, 0, half, 1)
-        quantize_w1(low0, 0, 0)
-        quantize_w1(high0, 0, 1)
-        for b in range(BLOCKS):
-            first_product(0, b)
-        w1_codes[1] = sb("w1_codes1", [P, H], U32, tag="high0")
-        low1 = sb("low1", shape, BF16)
-        high1 = sb("high1", shape, BF16, tag="low0")
-        for half in range(2):
-            cast_w1(nc.scalar.copy, low1, 1, half, 0)
-            cast_w1(nc.vector.tensor_copy, high1, 1, half, 1)
-        quantize_w1(low1, 1, 0)
-        quantize_w1(high1, 1, 1)
-        xw[1] = sb("xw1", [P, S], U32, tag="low1")
+        for z in range(PASSES):
+            w1_codes[z] = sb("w1_codes%d" % z, [P, H], U32)
+            low = sb("low%d" % z, [P, 2, P, PACK], BF16)
+            high = sb("high%d" % z, [P, 2, P, PACK], BF16)
+            for half in range(2):
+                cast_w1(nc.scalar.copy, low, z, half, 0)
+                cast_w1(nc.scalar.copy if (z, half) == (0, 0) else nc.vector.tensor_copy, high, z, half, 1)
+            quantize_w1(high, z, 1)
+            quantize_w1(low, z, 0)
+            if z == 0:
+                for b in range(BLOCKS):
+                    first_product(0, b)
+        xw[1] = sb("xw1", [P, S], U32)
         for b in range(BLOCKS):
             gather_x(1, b * BLOCK, BLOCK)
             first_product(1, b)
@@ -206,16 +179,24 @@ def tile_picked_modgate_mlpsilu_p_kernel(
             y_sb[b] = sb("y_sb%d" % b, [P, BLOCK], F32)
             nc.scalar.copy(y_sb[b][:], y[:])
 
+        g = {}
+
+        def gather_gate(half, tag):
+            g[half] = sb("g%d" % half, [P, S // 2], F32, tag=tag)
+            nc.vector.tensor_copy(g[half][:], gate_all[:].indirect(entries(half * S // 2, S // 2)))
+
         def scatter(b):
             nc.vector.tensor_tensor(
                 window[:].indirect(entries(b * BLOCK, BLOCK)),
                 y_sb[b][:],
-                g[:, b * BLOCK : (b + 1) * BLOCK],
+                g[b // 2][:, (b % 2) * BLOCK : (b % 2 + 1) * BLOCK],
                 MULT,
             )
 
+        gather_gate(0, None)
         silu_quant(0)
         silu_quant(1)
+        gather_gate(1, "h0")
         for b in range(BLOCKS):
             second_product(b)
             scatter(b)

@@ -37,7 +37,6 @@ def tile_picked_modgate_mlpsilu_p_kernel(
             return keep.tile(shape, dtype, name=name, tag=tag or name, align_bytes=64)
 
         offsets = sb("offsets", [P, S // 16], U16)
-        nc.sync.dma_start(offsets[:], offs)
 
         def entries(first, count):
             return offsets[:, first // 16 : (first + count) // 16]
@@ -68,12 +67,13 @@ def tile_picked_modgate_mlpsilu_p_kernel(
             xw_all[z] = words
 
         load_x(0)
-        load_w1(0, 0)
+        nc.sync.dma_start(offsets[:], offs)
         for q in range(4):
             nc.sync.dma_start(
                 xs_all[32 * q : 32 * q + 4 * PASSES, :].bitcast(I32),
                 x_scales[:, 4 * q : 4 * q + 4, :].bitcast(I32),
             )
+        load_w1(0, 0)
         load_w1(0, 1)
         load_w1(1, 0)
         load_w1(1, 1)

@@ -68,12 +68,12 @@ def tile_picked_modgate_mlpsilu_p_kernel(
 
         load_x(0)
         nc.sync.dma_start(offsets[:], offs)
+        load_w1(0, 0)
         for q in range(4):
             nc.sync.dma_start(
                 xs_all[32 * q : 32 * q + 4 * PASSES, :].bitcast(I32),
                 x_scales[:, 4 * q : 4 * q + 4, :].bitcast(I32),
             )
-        load_w1(0, 0)
         load_w1(0, 1)
         load_w1(1, 0)
         load_w1(1, 1)
@@ -88,7 +88,8 @@ def tile_picked_modgate_mlpsilu_p_kernel(
                 w2_scales[0, 4 * q : 4 * q + 4, :].bitcast(I32),
             )
 
-        xw = {}
+
+        xw = [sb("xw%d" % z, [P, S], U32) for z in range(PASSES)]
 
         def gather_x(z, first, count):
             nc.vector.tensor_copy(
@@ -96,32 +97,25 @@ def tile_picked_modgate_mlpsilu_p_kernel(
                 xw_all[z][:].bitcast(U32).indirect(entries(first, count)),
             )
 
-        xw[0] = sb("xw0", [P, S], U32)
         gather_x(0, 0, S)
+
         xs = sb("xs", [P, S], U8)
         nc.vector.tensor_copy(xs[:], xs_all[:].indirect(offsets[:]))
 
-        w1_codes = {}
+        w1_codes = [sb("w1_codes%d" % z, [P, H], U32) for z in range(PASSES)]
         w1_plane = [sb("w1_plane%d" % z, [P, H], U8) for z in range(PASSES)]
 
-        def cast_w1(copy, grouped, z, half, pair):
-            src = w1_raw[z, half][:].rearrange("p j (m t) -> p m j t", t=PACK)
-            dst = grouped[:, :, half * MH : (half + 1) * MH, :]
-            copy(dst.rearrange("p t m j -> p m j t"), src[:, :, :, 2 * pair : 2 * pair + 2])
-
-        def quantize_w1(grouped, z, pair):
-            cols = slice(pair * HALF, (pair + 1) * HALF)
+        def quantize_w1(z, first, count, grouped):
+            cols = slice(first, first + count)
             nc.vector.quantize_mx(
-                out=w1_codes[z][:, cols].bitcast(FP8X4),
-                scales=w1_plane[z][:, cols],
-                in_=grouped[:].rearrange("p t m j -> p (t m j)"),
+                out=w1_codes[z][:, cols].bitcast(FP8X4), scales=w1_plane[z][:, cols], in_=grouped
             )
 
         banks = [psum.tile([P, PACK, BLOCK], F32, name="h_bank%d" % b) for b in range(BLOCKS)]
 
         def first_product(z, b):
             tokens = slice(b * BLOCK, (b + 1) * BLOCK)
-            for t in (2, 3, 0, 1):
+            for t in range(PACK):
                 cols = slice(t * P, (t + 1) * P)
                 nc.tensor.matmul_mx(
                     out=banks[b][:, t, :],
@@ -129,33 +123,44 @@ def tile_picked_modgate_mlpsilu_p_kernel(
                     lhsT_scale=w1_plane[z][:, cols],
                     rhs=xw[z][:, tokens].bitcast(FP8X4),
                     rhs_scale=xs[4 * z : P, tokens],
-                    start=(z == 0 and t == 2),
-                    stop=(z == PASSES - 1 and t == 1),
+                    start=(z == 0 and t == 0),
+                    stop=(z == PASSES - 1 and t == PACK - 1),
                 )
 
-        for z in range(PASSES):
-            w1_codes[z] = sb("w1_codes%d" % z, [P, H], U32)
-            low = sb("low%d" % z, [P, 2, P, PACK], BF16)
-            high = sb("high%d" % z, [P, 2, P, PACK], BF16)
+        def dealt(z, half):
+            return w1_raw[z, half][:].rearrange("p j (m t) -> p m j t", t=PACK)
+
+        def round_and_quantize(z):
+            grouped = [sb("grouped%d%d" % (z, pair), [P, 2, P, PACK], BF16) for pair in range(2)]
             for half in range(2):
-                cast_w1(nc.scalar.copy, low, z, half, 0)
-                cast_w1(nc.scalar.copy if (z, half) == (0, 0) else nc.vector.tensor_copy, high, z, half, 1)
-            quantize_w1(high, z, 1)
-            quantize_w1(low, z, 0)
-            if z == 0:
-                for b in range(BLOCKS):
-                    first_product(0, b)
-        xw[1] = sb("xw1", [P, S], U32)
+                for pair in range(2):
+                    copy = nc.vector.tensor_copy if (half, pair) == (1, 0) else nc.scalar.copy
+                    copy(
+                        grouped[pair][:, :, half * MH : (half + 1) * MH, :].rearrange("p t m j -> p m j t"),
+                        dealt(z, half)[:, :, :, 2 * pair : 2 * pair + 2],
+                    )
+            for pair in range(2):
+                quantize_w1(z, pair * HALF, HALF, grouped[pair][:].rearrange("p t m j -> p (t m j)"))
+
+        round_and_quantize(0)
         for b in range(BLOCKS):
-            gather_x(1, b * BLOCK, BLOCK)
-            first_product(1, b)
+            first_product(0, b)
+        for half in range(2):
+            for pair, copy in ((0, nc.vector.tensor_copy), (1, nc.scalar.copy)):
+                grouped = sb("late%d%d" % (half, pair), [P, 2, MH, PACK], BF16)
+                copy(grouped[:].rearrange("p t m j -> p m j t"), dealt(1, half)[:, :, :, 2 * pair : 2 * pair + 2])
+                for u in range(2):
+                    quantize_w1(1, (2 * pair + u) * P + half * MH, MH, grouped[:, u].rearrange("p m j -> p (m j)"))
+        for first, count in ((0, 1), (2, 2), (1, 1)):
+            gather_x(1, first * BLOCK, count * BLOCK)
+            for b in range(first, first + count):
+                first_product(1, b)
 
         h_codes = {}
         h_plane = {}
-        y_sb = {}
 
         def silu_quant(b):
-            h = sb("h%d" % b, [P, BLOCK, PACK], BF16, tag="h_codes%d" % (b - 2) if b >= 2 else None)
+            h = sb("h%d" % b, [P, BLOCK, PACK], BF16, tag="h_codes0" if b == 1 else None)
             nc.scalar.activation(h[:], banks[b][:].rearrange("p t n -> p n t"), SILU)
             h_codes[b] = sb("h_codes%d" % b, [P, BLOCK], U32)
             h_plane[b] = sb("h_plane%d" % b, [P, BLOCK], U8)
@@ -165,41 +170,39 @@ def tile_picked_modgate_mlpsilu_p_kernel(
                 in_=h[:].rearrange("p n t -> p (n t)"),
             )
 
-        def second_product(b):
-            y = psum.tile([P, BLOCK], F32, name="y_bank%d" % b)
-            nc.tensor.matmul_mx(
-                out=y[:],
-                lhsT=w2_codes[:].bitcast(FP4X4),
-                lhsT_scale=w2_plane[:],
-                rhs=h_codes[b][:].bitcast(FP8X4),
-                rhs_scale=h_plane[b][:],
-                start=True,
-                stop=True,
-            )
-            y_sb[b] = sb("y_sb%d" % b, [P, BLOCK], F32)
-            nc.scalar.copy(y_sb[b][:], y[:])
+        def gather_gate(dst, first, count):
+            nc.vector.tensor_copy(dst, gate_all[:].indirect(entries(first * BLOCK, count * BLOCK)))
 
-        g = {}
-
-        def gather_gate(half, tag):
-            g[half] = sb("g%d" % half, [P, S // 2], F32, tag=tag)
-            nc.vector.tensor_copy(g[half][:], gate_all[:].indirect(entries(half * S // 2, S // 2)))
-
-        def scatter(b):
+        def second_product(first, count, g):
+            y = psum.tile([P, count * BLOCK], F32, name="y_bank%d" % first)
+            for i in range(count):
+                nc.tensor.matmul_mx(
+                    out=y[:, i * BLOCK : (i + 1) * BLOCK],
+                    lhsT=w2_codes[:].bitcast(FP4X4),
+                    lhsT_scale=w2_plane[:],
+                    rhs=h_codes[first + i][:].bitcast(FP8X4),
+                    rhs_scale=h_plane[first + i][:],
+                    start=True,
+                    stop=True,
+                )
+            y_sb = sb("y_sb%d" % first, [P, count * BLOCK], F32)
+            nc.scalar.copy(y_sb[:], y[:])
             nc.vector.tensor_tensor(
-                window[:].indirect(entries(b * BLOCK, BLOCK)),
-                y_sb[b][:],
-                g[b // 2][:, (b % 2) * BLOCK : (b % 2 + 1) * BLOCK],
+                window[:].indirect(entries(first * BLOCK, count * BLOCK)),
+                y_sb[:],
+                g,
                 MULT,
             )
 
-        gather_gate(0, None)
+        g01 = sb("g01", [P, 2 * BLOCK], F32)
+        gather_gate(g01[:], 0, 2)
         silu_quant(0)
+        g23 = sb("g23", [P, 2 * BLOCK], F32, tag="h0")
+        gather_gate(g23[:], 2, 2)
+        silu_quant(2)
+        silu_quant(3)
+        second_product(0, 1, g01[:, :BLOCK])
         silu_quant(1)
-        gather_gate(1, "h0")
-        for b in range(BLOCKS):
-            second_product(b)
-            scatter(b)
-            if b + 2 < BLOCKS:
-                silu_quant(b + 2)
+        second_product(2, 2, g23[:])
+        second_product(1, 1, g01[:, BLOCK:])
         nc.sync.dma_start(out, window[:])

@@ -22,7 +22,6 @@ PASSES = K // (P * PACK)
 BLOCK = 128
 BLOCKS = S // BLOCK
 HALF = H // 2
-MH = P // 2
 
 
 def tile_picked_modgate_mlpsilu_p_kernel(
@@ -55,11 +54,11 @@ def tile_picked_modgate_mlpsilu_p_kernel(
         w1_raw = {}
         xw_all = {}
 
-        def load_w1(z, half):
-            raw = sb("w1_raw%d%d" % (z, half), [P, PACK, HALF], F32)
-            rows = w1[z * P * PACK : (z + 1) * P * PACK, half * HALF : (half + 1) * HALF]
+        def load_w1(z):
+            raw = sb("w1_raw%d" % z, [P, PACK, H], F32)
+            rows = w1[z * P * PACK : (z + 1) * P * PACK, :]
             nc.sync.dma_start(raw[:], rows.rearrange("(p j) c -> p j c", j=PACK))
-            w1_raw[z, half] = raw
+            w1_raw[z] = raw
 
         def load_x(z):
             words = sb("xw_all%d" % z, [P, T], I32)
@@ -68,15 +67,13 @@ def tile_picked_modgate_mlpsilu_p_kernel(
 
         load_x(0)
         nc.sync.dma_start(offsets[:], offs)
-        load_w1(0, 0)
         for q in range(4):
             nc.sync.dma_start(
                 xs_all[32 * q : 32 * q + 4 * PASSES, :].bitcast(I32),
                 x_scales[:, 4 * q : 4 * q + 4, :].bitcast(I32),
             )
-        load_w1(0, 1)
-        load_w1(1, 0)
-        load_w1(1, 1)
+        load_w1(0)
+        load_w1(1)
         load_x(1)
         gate_all = sb("gate_all", [P, T], F32)
         nc.sync.dma_start(gate_all[:], gate)
@@ -113,9 +110,9 @@ def tile_picked_modgate_mlpsilu_p_kernel(
 
         banks = [psum.tile([P, PACK, BLOCK], F32, name="h_bank%d" % b) for b in range(BLOCKS)]
 
-        def first_product(z, b):
+        def first_product(z, b, slices):
             tokens = slice(b * BLOCK, (b + 1) * BLOCK)
-            for t in range(PACK):
+            for t in slices:
                 cols = slice(t * P, (t + 1) * P)
                 nc.tensor.matmul_mx(
                     out=banks[b][:, t, :],
@@ -127,34 +124,27 @@ def tile_picked_modgate_mlpsilu_p_kernel(
                     stop=(z == PASSES - 1 and t == PACK - 1),
                 )
 
-        def dealt(z, half):
-            return w1_raw[z, half][:].rearrange("p j (m t) -> p m j t", t=PACK)
+        def round_w1(z, pair):
+            grouped = sb("grouped%d%d" % (z, pair), [P, 2, P, PACK], BF16)
+            dealt = w1_raw[z][:].rearrange("p j (m t) -> p m j t", t=PACK)
+            copy = nc.vector.tensor_copy if pair == 0 else nc.scalar.copy
+            copy(grouped[:].rearrange("p t m j -> p m j t"), dealt[:, :, :, 2 * pair : 2 * pair + 2])
+            return grouped[:].rearrange("p t m j -> p (t m j)")
 
-        def round_and_quantize(z):
-            grouped = [sb("grouped%d%d" % (z, pair), [P, 2, P, PACK], BF16) for pair in range(2)]
-            for half in range(2):
-                for pair in range(2):
-                    copy = nc.vector.tensor_copy if (half, pair) == (1, 0) else nc.scalar.copy
-                    copy(
-                        grouped[pair][:, :, half * MH : (half + 1) * MH, :].rearrange("p t m j -> p m j t"),
-                        dealt(z, half)[:, :, :, 2 * pair : 2 * pair + 2],
-                    )
-            for pair in range(2):
-                quantize_w1(z, pair * HALF, HALF, grouped[pair][:].rearrange("p t m j -> p (t m j)"))
-
-        round_and_quantize(0)
-        for b in range(BLOCKS):
-            first_product(0, b)
-        for half in range(2):
-            for pair, copy in ((0, nc.vector.tensor_copy), (1, nc.scalar.copy)):
-                grouped = sb("late%d%d" % (half, pair), [P, 2, MH, PACK], BF16)
-                copy(grouped[:].rearrange("p t m j -> p m j t"), dealt(1, half)[:, :, :, 2 * pair : 2 * pair + 2])
-                for u in range(2):
-                    quantize_w1(1, (2 * pair + u) * P + half * MH, MH, grouped[:, u].rearrange("p m j -> p (m j)"))
-        for first, count in ((0, 1), (2, 2), (1, 1)):
+        rounded = [round_w1(0, pair) for pair in range(2)]
+        for pair in range(2):
+            quantize_w1(0, pair * HALF, HALF, rounded[pair])
+            for b in range(BLOCKS):
+                first_product(0, b, (2 * pair, 2 * pair + 1))
+        rounded = [round_w1(1, pair) for pair in range(2)]
+        quantize_w1(1, 0, HALF, rounded[0])
+        gather_x(1, 0, BLOCK)
+        quantize_w1(1, HALF, HALF, rounded[1])
+        first_product(1, 0, range(PACK))
+        for first, count in ((2, 2), (1, 1)):
             gather_x(1, first * BLOCK, count * BLOCK)
             for b in range(first, first + count):
-                first_product(1, b)
+                first_product(1, b, range(PACK))
 
         h_codes = {}
         h_plane = {}

@@ -99,6 +99,18 @@ def tile_picked_modgate_mlpsilu_p_kernel(
         xs = sb("xs", [P, S], U8)
         nc.vector.tensor_copy(xs[:], xs_all[:].indirect(offsets[:]))
 
+        warm_bank = psum.tile([P, S], F32, name="warm_bank")
+        for i in range(2):
+            nc.tensor.matmul_mx(
+                out=warm_bank[:],
+                lhsT=xw[0][:, :P].bitcast(FP8X4),
+                lhsT_scale=xs[:, :P],
+                rhs=xw[0][:].bitcast(FP8X4),
+                rhs_scale=xs[:],
+                start=True,
+                stop=True,
+            )
+
         w1_codes = [sb("w1_codes%d" % z, [P, H], U32) for z in range(PASSES)]
         w1_plane = [sb("w1_plane%d" % z, [P, H], U8) for z in range(PASSES)]
 
@@ -141,7 +153,7 @@ def tile_picked_modgate_mlpsilu_p_kernel(
         gather_x(1, 0, BLOCK)
         quantize_w1(1, HALF, HALF, rounded[1])
         first_product(1, 0, range(PACK))
-        for first, count in ((2, 2), (1, 1)):
+        for first, count in ((1, 1), (2, 2)):
             gather_x(1, first * BLOCK, count * BLOCK)
             for b in range(first, first + count):
                 first_product(1, b, range(PACK))
@@ -150,7 +162,7 @@ def tile_picked_modgate_mlpsilu_p_kernel(
         h_plane = {}
 
         def silu_quant(b):
-            h = sb("h%d" % b, [P, BLOCK, PACK], BF16, tag="h_codes0" if b == 1 else None)
+            h = sb("h%d" % b, [P, BLOCK, PACK], BF16, tag={2: "h_codes0", 3: "h_plane0"}.get(b))
             nc.scalar.activation(h[:], banks[b][:].rearrange("p t n -> p n t"), SILU)
             h_codes[b] = sb("h_codes%d" % b, [P, BLOCK], U32)
             h_plane[b] = sb("h_plane%d" % b, [P, BLOCK], U8)
@@ -189,10 +201,10 @@ def tile_picked_modgate_mlpsilu_p_kernel(
         silu_quant(0)
         g23 = sb("g23", [P, 2 * BLOCK], F32, tag="h0")
         gather_gate(g23[:], 2, 2)
+        silu_quant(1)
+        second_product(0, 1, g01[:, :BLOCK])
         silu_quant(2)
         silu_quant(3)
-        second_product(0, 1, g01[:, :BLOCK])
-        silu_quant(1)
-        second_product(2, 2, g23[:])
         second_product(1, 1, g01[:, BLOCK:])
+        second_product(2, 2, g23[:])
         nc.sync.dma_start(out, window[:])

@@ -22,6 +22,7 @@ PASSES = K // (P * PACK)
 BLOCK = 128
 BLOCKS = S // BLOCK
 HALF = H // 2
+MH = P // 2
 
 
 def tile_picked_modgate_mlpsilu_p_kernel(
@@ -99,18 +100,6 @@ def tile_picked_modgate_mlpsilu_p_kernel(
         xs = sb("xs", [P, S], U8)
         nc.vector.tensor_copy(xs[:], xs_all[:].indirect(offsets[:]))
 
-        warm_bank = psum.tile([P, S], F32, name="warm_bank")
-        for i in range(2):
-            nc.tensor.matmul_mx(
-                out=warm_bank[:],
-                lhsT=xw[0][:, :P].bitcast(FP8X4),
-                lhsT_scale=xs[:, :P],
-                rhs=xw[0][:].bitcast(FP8X4),
-                rhs_scale=xs[:],
-                start=True,
-                stop=True,
-            )
-
         w1_codes = [sb("w1_codes%d" % z, [P, H], U32) for z in range(PASSES)]
         w1_plane = [sb("w1_plane%d" % z, [P, H], U8) for z in range(PASSES)]
 
@@ -148,10 +137,22 @@ def tile_picked_modgate_mlpsilu_p_kernel(
             quantize_w1(0, pair * HALF, HALF, rounded[pair])
             for b in range(BLOCKS):
                 first_product(0, b, (2 * pair, 2 * pair + 1))
-        rounded = [round_w1(1, pair) for pair in range(2)]
-        quantize_w1(1, 0, HALF, rounded[0])
+        low = round_w1(1, 0)
+        dealt = w1_raw[1][:].rearrange("p j (m t) -> p m j t", t=PACK)
+        high = [sb("high%d" % half, [P, 2, MH, PACK], BF16) for half in range(2)]
+        for half in range(2):
+            nc.scalar.copy(
+                high[half][:].rearrange("p t m j -> p m j t"), dealt[:, half * MH : (half + 1) * MH, :, 2:4]
+            )
+
+        def quantize_high(half):
+            for u in range(2):
+                quantize_w1(1, (2 + u) * P + half * MH, MH, high[half][:, u].rearrange("p m j -> p (m j)"))
+
+        quantize_high(0)
+        quantize_w1(1, 0, HALF, low)
         gather_x(1, 0, BLOCK)
-        quantize_w1(1, HALF, HALF, rounded[1])
+        quantize_high(1)
         first_product(1, 0, range(PACK))
         for first, count in ((1, 1), (2, 2)):
             gather_x(1, first * BLOCK, count * BLOCK)

@@ -14,6 +14,7 @@ U8 = mybir.dt.uint8
 FP8X4 = mybir.dt.float8_e4m3fn_x4
 FP4X4 = mybir.dt.float4_e2m1fn_x4
 SILU = mybir.ActivationFunctionType.Silu
+COPY = mybir.ActivationFunctionType.Copy
 MULT = mybir.AluOpType.mult
 
 P = 128
@@ -159,53 +160,54 @@ def tile_picked_modgate_mlpsilu_p_kernel(
             for b in range(first, first + count):
                 first_product(1, b, range(PACK))
 
-        h_codes = {}
-        h_plane = {}
+        def silu(b, dst):
+            nc.scalar.activation(dst, banks[b][:].rearrange("p t n -> p n t"), SILU)
 
-        def silu_quant(b):
-            h = sb("h%d" % b, [P, BLOCK, PACK], BF16, tag={2: "h_codes0", 3: "h_plane0"}.get(b))
-            nc.scalar.activation(h[:], banks[b][:].rearrange("p t n -> p n t"), SILU)
-            h_codes[b] = sb("h_codes%d" % b, [P, BLOCK], U32)
-            h_plane[b] = sb("h_plane%d" % b, [P, BLOCK], U8)
+        def quantize_h(name, h, count, tag):
+            codes = sb("h_codes" + name, [P, count], U32, tag=tag)
+            plane = sb("h_plane" + name, [P, count], U8)
             nc.vector.quantize_mx(
-                out=h_codes[b][:].bitcast(FP8X4),
-                scales=h_plane[b][:],
-                in_=h[:].rearrange("p n t -> p (n t)"),
+                out=codes[:].bitcast(FP8X4), scales=plane[:], in_=h[:].rearrange("p n t -> p (n t)")
             )
+            return codes, plane
 
-        def gather_gate(dst, first, count):
-            nc.vector.tensor_copy(dst, gate_all[:].indirect(entries(first * BLOCK, count * BLOCK)))
-
-        def second_product(first, count, g):
-            y = psum.tile([P, count * BLOCK], F32, name="y_bank%d" % first)
-            for i in range(count):
-                nc.tensor.matmul_mx(
-                    out=y[:, i * BLOCK : (i + 1) * BLOCK],
-                    lhsT=w2_codes[:].bitcast(FP4X4),
-                    lhsT_scale=w2_plane[:],
-                    rhs=h_codes[first + i][:].bitcast(FP8X4),
-                    rhs_scale=h_plane[first + i][:],
-                    start=True,
-                    stop=True,
-                )
-            y_sb = sb("y_sb%d" % first, [P, count * BLOCK], F32)
-            nc.scalar.copy(y_sb[:], y[:])
-            nc.vector.tensor_tensor(
-                window[:].indirect(entries(first * BLOCK, count * BLOCK)),
-                y_sb[:],
-                g,
-                MULT,
+        def second_product(name, quantized, count):
+            codes, plane = quantized
+            y = psum.tile([P, count], F32, name="y_bank" + name)
+            nc.tensor.matmul_mx(
+                out=y[:],
+                lhsT=w2_codes[:].bitcast(FP4X4),
+                lhsT_scale=w2_plane[:],
+                rhs=codes[:].bitcast(FP8X4),
+                rhs_scale=plane[:],
+                start=True,
+                stop=True,
             )
+            return y
 
-        g01 = sb("g01", [P, 2 * BLOCK], F32)
-        gather_gate(g01[:], 0, 2)
-        silu_quant(0)
-        g23 = sb("g23", [P, 2 * BLOCK], F32, tag="h0")
-        gather_gate(g23[:], 2, 2)
-        silu_quant(1)
-        second_product(0, 1, g01[:, :BLOCK])
-        silu_quant(2)
-        silu_quant(3)
-        second_product(1, 1, g01[:, BLOCK:])
-        second_product(2, 2, g23[:])
+        g0 = sb("g0", [P, BLOCK], F32)
+        nc.vector.tensor_copy(g0[:], gate_all[:].indirect(entries(0, BLOCK)))
+        g1 = sb("g1", [P, BLOCK], F32)
+        nc.vector.tensor_copy(g1[:], gate_all[:].indirect(entries(BLOCK, BLOCK)))
+        h0 = sb("h0", [P, BLOCK, PACK], BF16)
+        silu(0, h0[:])
+        y0 = second_product("0", quantize_h("0", h0, BLOCK, None), BLOCK)
+        weighted = sb("weighted", [P, BLOCK], F32)
+        nc.vector.tensor_tensor(weighted[:], y0[:], g0[:], MULT)
+        h1 = sb("h1", [P, BLOCK, PACK], BF16)
+        silu(1, h1[:])
+        y1 = second_product("1", quantize_h("1", h1, BLOCK, "h_codes0"), BLOCK)
+        nc.vector.tensor_copy(window[:].indirect(entries(0, BLOCK)), weighted[:])
+        h23 = sb("h23", [P, 2 * BLOCK, PACK], BF16)
+        silu(2, h23[:, :BLOCK, :])
+        silu(3, h23[:, BLOCK:, :])
+        y23 = second_product("23", quantize_h("23", h23, 2 * BLOCK, "g0"), 2 * BLOCK)
+        y_sb1 = sb("y_sb1", [P, BLOCK], F32)
+        nc.scalar.copy(y_sb1[:], y1[:])
+        nc.vector.tensor_tensor(window[:].indirect(entries(BLOCK, BLOCK)), y_sb1[:], g1[:], MULT)
+        g23 = sb("g23", [P, 2 * BLOCK], F32, tag="h_codes0")
+        nc.scalar.activation(g23[:], gate_all[:].indirect(entries(2 * BLOCK, 2 * BLOCK)), COPY)
+        y_sb23 = sb("y_sb23", [P, 2 * BLOCK], F32)
+        nc.scalar.copy(y_sb23[:], y23[:])
+        nc.vector.tensor_tensor(window[:].indirect(entries(2 * BLOCK, 2 * BLOCK)), y_sb23[:], g23[:], MULT)
         nc.sync.dma_start(out, window[:])

@@ -187,11 +187,11 @@ def tile_picked_modgate_mlpsilu_p_kernel(
 
         g0 = sb("g0", [P, BLOCK], F32)
         nc.vector.tensor_copy(g0[:], gate_all[:].indirect(entries(0, BLOCK)))
-        g1 = sb("g1", [P, BLOCK], F32)
-        nc.vector.tensor_copy(g1[:], gate_all[:].indirect(entries(BLOCK, BLOCK)))
         h0 = sb("h0", [P, BLOCK, PACK], BF16)
         silu(0, h0[:])
         y0 = second_product("0", quantize_h("0", h0, BLOCK, None), BLOCK)
+        g1 = sb("g1", [P, BLOCK], F32, tag="h0")
+        nc.vector.tensor_copy(g1[:], gate_all[:].indirect(entries(BLOCK, BLOCK)))
         weighted = sb("weighted", [P, BLOCK], F32)
         nc.vector.tensor_tensor(weighted[:], y0[:], g0[:], MULT)
         h1 = sb("h1", [P, BLOCK, PACK], BF16)

from contextlib import ExitStack

import concourse.mybir as mybir

K, T, S, H, N = 1024, 1024, 512, 512, 128
FLOPS = 2 * K * H * S + 2 * H * N * S

F32 = mybir.dt.float32
BF16 = mybir.dt.bfloat16
I32 = mybir.dt.int32
U32 = mybir.dt.uint32
U16 = mybir.dt.uint16
U8 = mybir.dt.uint8
FP8X4 = mybir.dt.float8_e4m3fn_x4
FP4X4 = mybir.dt.float4_e2m1fn_x4
SILU = mybir.ActivationFunctionType.Silu
COPY = mybir.ActivationFunctionType.Copy
MULT = mybir.AluOpType.mult

P = 128
PACK = 4
PASSES = K // (P * PACK)
BLOCK = 128
BLOCKS = S // BLOCK
HALF = H // 2
MH = P // 2


def tile_picked_modgate_mlpsilu_p_kernel(
    tc, x_words, x_scales, gate, w1, w2_words, w2_scales, offs, out
):
    nc = tc.nc
    with ExitStack() as ctx:
        keep = ctx.enter_context(tc.tile_pool(name="keep", bufs=1))
        psum = ctx.enter_context(tc.psum_pool(name="psum", bufs=1))

        def sb(name, shape, dtype, tag=None):
            return keep.tile(shape, dtype, name=name, tag=tag or name, align_bytes=64)

        offsets = sb("offsets", [P, S // 16], U16)

        def entries(first, count):
            return offsets[:, first // 16 : (first + count) // 16]

        xs_all = sb("xs_all", [P, T], U8)
        nc.vector.memset(xs_all[:].bitcast(I32), 0)
        warm_in = sb("warm_in", [P, 1], F32)
        warm_out = sb("warm_out", [P, 1], F32)
        nc.gpsimd.memset(warm_in[:], 0.0)
        nc.scalar.activation(warm_out[:], warm_in[:], SILU)
        w2_plane = sb("w2_plane", [P, N], U8)
        nc.vector.memset(w2_plane[:].bitcast(I32), 0)
        window = sb("window", [P, T], F32)
        nc.vector.memset(window[:], 0.0)

        w1_raw = {}
        xw_all = {}

        def load_w1(z):
            raw = sb("w1_raw%d" % z, [P, PACK, H], F32)
            rows = w1[z * P * PACK : (z + 1) * P * PACK, :]
            nc.sync.dma_start(raw[:], rows.rearrange("(p j) c -> p j c", j=PACK))
            w1_raw[z] = raw

        def load_x(z):
            words = sb("xw_all%d" % z, [P, T], I32)
            nc.sync.dma_start(words[:], x_words[z].rearrange("p n t -> p (n t)").bitcast(I32))
            xw_all[z] = words

        load_x(0)
        nc.sync.dma_start(offsets[:], offs)
        for q in range(4):
            nc.sync.dma_start(
                xs_all[32 * q : 32 * q + 4 * PASSES, :].bitcast(I32),
                x_scales[:, 4 * q : 4 * q + 4, :].bitcast(I32),
            )
        load_w1(0)
        load_w1(1)
        load_x(1)
        gate_all = sb("gate_all", [P, T], F32)
        nc.sync.dma_start(gate_all[:], gate)
        w2_codes = sb("w2_codes", [P, 2 * N], U8)
        nc.sync.dma_start(w2_codes[:].bitcast(I32), w2_words[0].bitcast(I32))
        for q in range(4):
            nc.sync.dma_start(
                w2_plane[32 * q : 32 * q + 4, :].bitcast(I32),
                w2_scales[0, 4 * q : 4 * q + 4, :].bitcast(I32),
            )


        xw = [sb("xw%d" % z, [P, S], U32) for z in range(PASSES)]

        def gather_x(z, first, count):
            nc.vector.tensor_copy(
                xw[z][:, first : first + count],
                xw_all[z][:].bitcast(U32).indirect(entries(first, count)),
            )

        gather_x(0, 0, S)

        xs = sb("xs", [P, S], U8)
        nc.vector.tensor_copy(xs[:], xs_all[:].indirect(offsets[:]))

        w1_codes = [sb("w1_codes%d" % z, [P, H], U32) for z in range(PASSES)]
        w1_plane = [sb("w1_plane%d" % z, [P, H], U8) for z in range(PASSES)]

        def quantize_w1(z, first, count, grouped):
            cols = slice(first, first + count)
            nc.vector.quantize_mx(
                out=w1_codes[z][:, cols].bitcast(FP8X4), scales=w1_plane[z][:, cols], in_=grouped
            )

        banks = [psum.tile([P, PACK, BLOCK], F32, name="h_bank%d" % b) for b in range(BLOCKS)]

        def first_product(z, b, slices):
            tokens = slice(b * BLOCK, (b + 1) * BLOCK)
            for t in slices:
                cols = slice(t * P, (t + 1) * P)
                nc.tensor.matmul_mx(
                    out=banks[b][:, t, :],
                    lhsT=w1_codes[z][:, cols].bitcast(FP8X4),
                    lhsT_scale=w1_plane[z][:, cols],
                    rhs=xw[z][:, tokens].bitcast(FP8X4),
                    rhs_scale=xs[4 * z : P, tokens],
                    start=(z == 0 and t == 0),
                    stop=(z == PASSES - 1 and t == PACK - 1),
                )

        def round_w1(z, pair):
            grouped = sb("grouped%d%d" % (z, pair), [P, 2, P, PACK], BF16)
            dealt = w1_raw[z][:].rearrange("p j (m t) -> p m j t", t=PACK)
            copy = nc.vector.tensor_copy if pair == 0 else nc.scalar.copy
            copy(grouped[:].rearrange("p t m j -> p m j t"), dealt[:, :, :, 2 * pair : 2 * pair + 2])
            return grouped[:].rearrange("p t m j -> p (t m j)")

        rounded = [round_w1(0, pair) for pair in range(2)]
        for pair in range(2):
            quantize_w1(0, pair * HALF, HALF, rounded[pair])
            for b in range(BLOCKS):
                first_product(0, b, (2 * pair, 2 * pair + 1))
        low = round_w1(1, 0)
        dealt = w1_raw[1][:].rearrange("p j (m t) -> p m j t", t=PACK)
        high = [sb("high%d" % half, [P, 2, MH, PACK], BF16) for half in range(2)]
        for half in range(2):
            nc.scalar.copy(
                high[half][:].rearrange("p t m j -> p m j t"), dealt[:, half * MH : (half + 1) * MH, :, 2:4]
            )

        def quantize_high(half):
            for u in range(2):
                quantize_w1(1, (2 + u) * P + half * MH, MH, high[half][:, u].rearrange("p m j -> p (m j)"))

        quantize_high(0)
        quantize_w1(1, 0, HALF, low)
        gather_x(1, 0, BLOCK)
        quantize_high(1)
        first_product(1, 0, range(PACK))
        for first, count in ((1, 1), (2, 2)):
            gather_x(1, first * BLOCK, count * BLOCK)
            for b in range(first, first + count):
                first_product(1, b, range(PACK))

        def silu(b, dst):
            nc.scalar.activation(dst, banks[b][:].rearrange("p t n -> p n t"), SILU)

        def quantize_h(name, h, count, tag):
            codes = sb("h_codes" + name, [P, count], U32, tag=tag)
            plane = sb("h_plane" + name, [P, count], U8)
            nc.vector.quantize_mx(
                out=codes[:].bitcast(FP8X4), scales=plane[:], in_=h[:].rearrange("p n t -> p (n t)")
            )
            return codes, plane

        def second_product(name, quantized, count):
            codes, plane = quantized
            y = psum.tile([P, count], F32, name="y_bank" + name)
            nc.tensor.matmul_mx(
                out=y[:],
                lhsT=w2_codes[:].bitcast(FP4X4),
                lhsT_scale=w2_plane[:],
                rhs=codes[:].bitcast(FP8X4),
                rhs_scale=plane[:],
                start=True,
                stop=True,
            )
            return y

        g0 = sb("g0", [P, BLOCK], F32)
        nc.vector.tensor_copy(g0[:], gate_all[:].indirect(entries(0, BLOCK)))
        h0 = sb("h0", [P, BLOCK, PACK], BF16)
        silu(0, h0[:])
        y0 = second_product("0", quantize_h("0", h0, BLOCK, None), BLOCK)
        g1 = sb("g1", [P, BLOCK], F32, tag="h0")
        nc.vector.tensor_copy(g1[:], gate_all[:].indirect(entries(BLOCK, BLOCK)))
        weighted = sb("weighted", [P, BLOCK], F32)
        nc.vector.tensor_tensor(weighted[:], y0[:], g0[:], MULT)
        h1 = sb("h1", [P, BLOCK, PACK], BF16)
        silu(1, h1[:])
        y1 = second_product("1", quantize_h("1", h1, BLOCK, "h_codes0"), BLOCK)
        nc.vector.tensor_copy(window[:].indirect(entries(0, BLOCK)), weighted[:])
        h23 = sb("h23", [P, 2 * BLOCK, PACK], BF16)
        silu(2, h23[:, :BLOCK, :])
        silu(3, h23[:, BLOCK:, :])
        y23 = second_product("23", quantize_h("23", h23, 2 * BLOCK, "g0"), 2 * BLOCK)
        y_sb1 = sb("y_sb1", [P, BLOCK], F32)
        nc.scalar.copy(y_sb1[:], y1[:])
        nc.vector.tensor_tensor(window[:].indirect(entries(BLOCK, BLOCK)), y_sb1[:], g1[:], MULT)
        g23 = sb("g23", [P, 2 * BLOCK], F32, tag="h_codes0")
        nc.scalar.activation(g23[:], gate_all[:].indirect(entries(2 * BLOCK, 2 * BLOCK)), COPY)
        y_sb23 = sb("y_sb23", [P, 2 * BLOCK], F32)
        nc.scalar.copy(y_sb23[:], y23[:])
        nc.vector.tensor_tensor(window[:].indirect(entries(2 * BLOCK, 2 * BLOCK)), y_sb23[:], g23[:], MULT)
        nc.sync.dma_start(out, window[:])
